import numpy as np
import ml_dtypes


def mxq(x, axis, fmt="e4m3"):
    dtype, down = {"e4m3": (ml_dtypes.float8_e4m3fn, 7), "e5m2": (ml_dtypes.float8_e5m2, 14)}[fmt]
    v = np.moveaxis(np.asarray(x, np.float32).astype(ml_dtypes.bfloat16).astype(np.float64), axis, -1)
    blocks = v.reshape(v.shape[:-1] + (-1, 32))
    amax = np.abs(blocks).max(-1, keepdims=True)
    byte = np.maximum(np.where(amax > 0, np.frexp(amax)[1] - 1 + 127, 0) - down, 1)
    scale = np.exp2(byte - 127.0)
    codes = (blocks / scale).astype(np.float32).astype(dtype).astype(np.float64)
    return np.moveaxis((codes * scale).reshape(v.shape), -1, axis)


WIDE = False


def mx_kscale(k):
    if not WIDE:
        return np.ones(k)
    levels = np.array([10, -10, 5, -5, 0])
    if k % 512:
        return np.exp2(np.random.permutation(np.resize(levels, k // 32))).repeat(32)
    a = np.empty((k // 512, 16))
    for p in range(k // 512):
        a[p, :8] = np.random.permutation(np.resize(levels, 8))
        for g in range(8):
            far = levels[np.abs(levels - a[p, g]) >= 10]
            a[p, g + 8] = far[np.random.randint(len(far))]
    return np.exp2(a.ravel()).repeat(32)


def f64(x):
    return np.asarray(x).astype(np.float64)


def striped(idx):
    return np.tile(idx.reshape(-1, 16).T, (8, 1)).astype(np.uint16)


def unstriped(offs):
    return offs[:16].T.reshape(-1).astype(np.int64)


E2M1 = np.array([0.0, 0.5, 1.0, 1.5, 2.0, 3.0, 4.0, 6.0, -0.0, -0.5, -1.0, -1.5, -2.0, -3.0, -4.0, -6.0])


def pack_weight(w, fmt):
    k, n = w.shape
    w = f64(np.asarray(w, np.float32).astype(ml_dtypes.bfloat16)).reshape(k // 32, 32, n)
    amax = np.abs(w).max(1)
    if fmt == "e4m3":
        byte = np.frexp(amax)[1] - 1 + 127 - 7
    else:
        mant, ex = np.frexp(amax / 6.0)
        byte = np.where(mant > 0.5, ex, ex - 1) + 127
    byte = np.clip(np.where(amax > 0, byte, 1), 1, 254)
    scaled = (w * np.exp2(127.0 - byte)[:, None, :]).reshape(k, n).astype(np.float32)
    by_word = np.ascontiguousarray(scaled.reshape(k // 512, 128, 4, n).transpose(0, 1, 3, 2))
    if fmt == "e4m3":
        words = by_word.astype(ml_dtypes.float8_e4m3fn).view(np.uint8)
    else:
        c = by_word.astype(ml_dtypes.float4_e2m1fn).view(np.uint8) & 0xF
        words = (c[..., 0::2] | (c[..., 1::2] << 4)).reshape(k // 512, 128, 2 * n)
    return np.ascontiguousarray(words), np.ascontiguousarray(byte.astype(np.uint8).reshape(k // 512, 16, n))


def unpack_weight(words, scales, fmt):
    g, _, n = scales.shape
    words = np.ascontiguousarray(words).reshape(g, 128, n, -1)
    if fmt == "e4m3":
        vals = words.view(ml_dtypes.float8_e4m3fn).astype(np.float64)
    else:
        nib = np.empty((g, 128, n, 4), np.uint8)
        nib[..., 0::2] = words & 0xF
        nib[..., 1::2] = words >> 4
        vals = E2M1[nib]
    vals = vals * np.repeat(np.exp2(scales.astype(np.float64) - 127.0), 8, axis=1)[..., None]
    return vals.transpose(0, 1, 3, 2).reshape(g * 512, n)


def gelu(v):
    return 0.5 * v * (1.0 + np.tanh(np.sqrt(2.0 / np.pi) * (v + 0.044715 * v**3)))


K, K4, K1, H, T, S, T3, S2, P = 1536, 1024, 512, 1024, 4096, 1024, 2048, 512, 512

def setup_inputs():
    n = np.random.standard_normal
    s = mx_kscale(K)[:, None]
    u = mx_kscale(H)[:, None]
    tab_words, tab_scales = pack_weight(n((K, T)) * s, "e4m3")
    tab2_words, tab2_scales = pack_weight(n((H, T3)) / np.sqrt(H) / u, "e4m3")
    w4_words, w4_scales = pack_weight(1.5 * n((K4, H)) / np.sqrt(K) / s[:K4], "e2m1")
    w1 = (1.5 * n((K1, H)) / np.sqrt(K) / s[K4:]).astype(np.float32)
    gain = (np.random.uniform(0.5, 1.2, H) * u[:, 0]).astype(np.float32)
    tol = n(S2).astype(np.float32)
    lean = (0.35 * n((S2, P))).astype(np.float32)
    return {"tab_words": tab_words, "tab_scales": tab_scales,
            "tab2_words": tab2_words, "tab2_scales": tab2_scales,
            "offs": striped(np.random.permutation(T)[:S]),
            "offs2": striped(np.random.permutation(T3)[:S2]),
            "pos1": striped(np.random.permutation(S)[:P]),
            "pos2": striped(np.random.permutation(S)[:P]),
            "w4_words": w4_words, "w4_scales": w4_scales,
            "w1": w1, "gain": gain, "tol": tol, "lean": lean}

def reference(tab_words, tab_scales, tab2_words, tab2_scales, offs, offs2, pos1, pos2,
              w4_words, w4_scales, w1, gain, tol, lean):
    v = unpack_weight(tab_words, tab_scales, "e4m3")[:, unstriped(offs)]
    v2 = unpack_weight(tab2_words, tab2_scales, "e4m3")[:, unstriped(offs2)]
    w4 = unpack_weight(w4_words, w4_scales, "e2m1")
    w1q = mxq(f64(w1), 0, "e4m3")
    z = w4.T @ v[:K4] + w1q.T @ v[K4:]
    h = z / (1.0 + np.exp(-z)) * f64(gain)[:, None]
    hq = mxq(h, 0, "e4m3")
    e = v2.T @ hq
    a = 1.0 / (1.0 + np.exp(-(e[:, unstriped(pos1)] + f64(tol)[:, None])))
    c = e[:, unstriped(pos2)]
    return (a + f64(lean)) * c

@@ -1,0 +1,242 @@
+from contextlib import ExitStack
+
+import concourse.mybir as mybir
+
+K, K4, K1, H, T, S, T3, S2, NP = 1536, 1024, 512, 1024, 4096, 1024, 2048, 512, 512
+FLOPS = 2 * K * H * S + 2 * H * S2 * S
+
+F32 = mybir.dt.float32
+BF16 = mybir.dt.bfloat16
+I32 = mybir.dt.int32
+U32 = mybir.dt.uint32
+U16 = mybir.dt.uint16
+U8 = mybir.dt.uint8
+FP8X4 = mybir.dt.float8_e4m3fn_x4
+FP4X4 = mybir.dt.float4_e2m1fn_x4
+ACT = mybir.ActivationFunctionType
+ALU = mybir.AluOpType
+
+P = 128
+JB = 128
+
+
+def tile_list_arbitrator_appointment_scores_kernel(
+    tc, tab_words, tab_scales, tab2_words, tab2_scales, offs, offs2, pos1, pos2,
+    w4_words, w4_scales, w1, gain, tol, lean, out,
+):
+    nc = tc.nc
+    with ExitStack() as ctx:
+        keep = ctx.enter_context(tc.tile_pool(name="keep", bufs=1))
+        stage = ctx.enter_context(tc.tile_pool(name="stage", bufs=1))
+        ring = ctx.enter_context(tc.tile_pool(name="ring", bufs=3))
+        psum = ctx.enter_context(tc.psum_pool(name="psum", bufs=8))
+
+        def held(name, shape, dtype):
+            return keep.tile(shape, dtype, name=name, align_bytes=64)
+
+        def staged(name, shape, dtype, kib):
+            return stage.tile(shape, dtype, name=name, align_bytes=64, offset=1024 * kib)
+
+        def words_of(table, a):
+            return table[a].rearrange("p t i -> p (t i)").bitcast(I32)
+
+        idx = keep.tile([P, S // 16], U16, name="idx")
+        idx2 = keep.tile([P, S2 // 16], U16, name="idx2")
+        p1 = keep.tile([P, NP // 16], U16, name="p1")
+        p2 = keep.tile([P, NP // 16], U16, name="p2")
+
+        v_scale_win = staged("v_scale_win", [P, T], U8, 40)
+        w4_scale_raw = staged("w4_scale_raw", [P, 2, H], U8, 48)
+        v2_scale_win = held("v2_scale_win", [P, T3], U8)
+        v_scale_1 = held("v_scale_1", [P, S], U8)
+        nc.vector.memset(v_scale_win[:].bitcast(I32), 0)
+        nc.vector.memset(w4_scale_raw[:].bitcast(I32), 0)
+        nc.vector.memset(v2_scale_win[:].bitcast(I32), 0)
+        nc.vector.memset(v_scale_1[:].bitcast(I32), 0)
+
+        v_win = [staged("v_win%d" % a, [P, T], U32, 16 * (a % 2)) for a in range(3)]
+        v2_win = [staged("v2_win%d" % b, [P, T3], U32, 16 + 8 * b) for b in range(2)]
+        w1_raw = [staged("w1_raw%d" % b, [P, 4, 512], F32, 32 + 8 * b) for b in range(2)]
+        w4_raw = staged("w4_raw", [P, 2, H], U16, 30)
+        lean_sb = staged("lean_sb", [P, 4, NP], F32, 32)
+        gain_sb = staged("gain_sb", [P, 2, 4], F32, 48)
+        tol_sb = staged("tol_sb", [P, 4], F32, 49)
+
+        def load_w1(b):
+            nc.sync.dma_start(
+                w1_raw[b][:], w1[:, 512 * b : 512 * (b + 1)].rearrange("(p j) c -> p j c", j=4))
+
+        nc.sync.dma_start(idx[:], offs)
+        nc.sync.dma_start(idx2[:], offs2)
+        nc.sync.dma_start(p1[:], pos1)
+        nc.sync.dma_start(p2[:], pos2)
+        nc.sync.dma_start(w4_raw[:].bitcast(I32), w4_words.rearrange("a p n -> p a n").bitcast(I32))
+        nc.sync.dma_start(v_win[0][:].bitcast(I32), words_of(tab_words, 0))
+        for q in range(4):
+            nc.scalar.dma_start(
+                v_scale_win[32 * q : 32 * q + 12, :].bitcast(I32),
+                tab_scales[:, 4 * q : 4 * q + 4, :].bitcast(I32))
+        for q in range(4):
+            (nc.scalar if q < 2 else nc.gpsimd).dma_start(
+                w4_scale_raw[32 * q : 32 * q + 4, :, :].bitcast(I32),
+                w4_scales[:, 4 * q : 4 * q + 4, :].rearrange("a r n -> r a n").bitcast(I32))
+        for q in range(4):
+            nc.gpsimd.dma_start(
+                v2_scale_win[32 * q : 32 * q + 8, :].bitcast(I32),
+                tab2_scales[:, 4 * q : 4 * q + 4, :].bitcast(I32))
+
+        w4_codes = held("w4_codes", [P, 4, 4, P], U16)
+        w4_plane = held("w4_plane", [P, 4, 4, P], U8)
+        nc.vector.tensor_copy(
+            w4_codes[:].rearrange("p g t q -> p g q t"),
+            w4_raw[:].rearrange("p a (b q t) -> p (a b) q t", b=2, t=4))
+        nc.sync.dma_start(v_win[1][:].bitcast(I32), words_of(tab_words, 1))
+        load_w1(0)
+
+        v_scale = held("v_scale", [P, S], U8)
+
+        v_codes = [held("v_codes%d" % a, [P, S], U32) for a in range(3)]
+
+        def gather_v(a, width):
+            for c0 in range(0, S, width):
+                nc.vector.tensor_copy(
+                    v_codes[a][:, c0 : c0 + width],
+                    v_win[a][:].indirect(idx[:, c0 // 16 : (c0 + width) // 16]))
+
+        w1_bf = [held("w1_bf%d" % b, [P, 4, P, 4], BF16) for b in range(2)]
+        w1_codes = [held("w1_codes%d" % b, [P, 512], U32) for b in range(2)]
+        w1_plane = [held("w1_plane%d" % b, [P, 512], U8) for b in range(2)]
+
+        def round_w1(b, halves):
+            width = P // halves
+            for m0 in range(0, P, width):
+                nc.scalar.copy(
+                    w1_bf[b][:, :, m0 : m0 + width, :].rearrange("p t m j -> p m j t"),
+                    w1_raw[b][:, :, 4 * m0 : 4 * (m0 + width)].rearrange("p j (m t) -> p m j t", t=4))
+
+        def quantise_w1(b):
+            nc.vector.quantize_mx(
+                w1_codes[b][:].bitcast(FP8X4), w1_plane[b][:],
+                w1_bf[b][:].rearrange("p t m j -> p (t m j)"))
+
+        v2_codes = [held("v2_codes%d" % b, [P, S2], U32) for b in range(2)]
+        v2_scale = held("v2_scale", [P, S2], U8)
+
+        def z_pass(bank, b, jb, a):
+            cols = slice(JB * jb, JB * (jb + 1))
+            for t in range(4):
+                if a < 2:
+                    lhsT = w4_codes[:, 2 * a + b, t, :].bitcast(FP4X4)
+                    lhsT_scale = w4_plane[:, 2 * a + b, t, :]
+                    rhs_scale = (v_scale if a == 0 else v_scale_1)[:, cols]
+                else:
+                    lhsT = w1_codes[b][:, P * t : P * (t + 1)].bitcast(FP8X4)
+                    lhsT_scale = w1_plane[b][:, P * t : P * (t + 1)]
+                    rhs_scale = v_scale[8:P, cols]
+                nc.tensor.matmul_mx(
+                    bank[:, JB * t : JB * (t + 1)], lhsT=lhsT, lhsT_scale=lhsT_scale,
+                    rhs=v_codes[a][:, cols].bitcast(FP8X4), rhs_scale=rhs_scale,
+                    start=(a == 0 and t == 0), stop=(a == 2 and t == 3))
+
+        gather_v(0, 512)
+        nc.sync.dma_start(v_win[2][:].bitcast(I32), words_of(tab_words, 2))
+        nc.vector.tensor_copy(v_scale[:], v_scale_win[:].indirect(idx[:]))
+        nc.scalar.dma_start(v_scale_1[0:100, :].bitcast(I32), v_scale[4:104, :].bitcast(I32))
+        load_w1(1)
+
+        nc.vector.tensor_copy(
+            w4_plane[:].rearrange("p g t q -> p g q t"),
+            w4_scale_raw[:].rearrange("p a (b q t) -> p (a b) q t", b=2, t=4))
+        nc.sync.dma_start(gain_sb[:], gain.rearrange("(b p t) -> p b t", b=2, t=4))
+        with nc.allow_non_contiguous_dma(reason="one value of tol for each partition"):
+            nc.sync.dma_start(tol_sb[:], tol.rearrange("(m p) -> p m", m=4))
+
+
+        z_banks = [psum.tile([P, 512], F32, name="bank", tag="bank") for jb in range(8)]
+        for jb in range(8):
+            z_pass(z_banks[jb], 0, jb, 0)
+        gather_v(1, 512)
+        for b in range(2):
+            nc.sync.dma_start(v2_win[b][:].bitcast(I32), words_of(tab2_words, b))
+        for jb in range(8):
+            z_pass(z_banks[jb], 0, jb, 1)
+        nc.vector.tensor_copy(v2_scale[:], v2_scale_win[:].indirect(idx2[:]))
+        round_w1(0, 1)
+        nc.sync.dma_start(lean_sb[:], lean.rearrange("(m p) n -> p m n", m=4))
+        quantise_w1(0)
+        gather_v(2, 256)
+
+        h_codes = [[held("h_codes%d%d" % (b, jh), [P, 512], U32) for jh in range(2)] for b in range(2)]
+        h_plane = [[held("h_plane%d%d" % (b, jh), [P, 512], U8) for jh in range(2)] for b in range(2)]
+        e_sb = [held("e_sb%d" % m, [P, S], F32) for m in range(4)]
+
+        def silu(bank):
+            s = ring.tile([P, JB, 4], F32, name="silu", tag="silu")
+            nc.scalar.activation(s[:], bank[:].rearrange("p (t j) -> p j t", t=4), ACT.Silu)
+            return s
+
+        def scale(s, b, h_bf, half):
+            nc.vector.tensor_tensor(
+                h_bf[:, JB * half : JB * (half + 1), :], s[:],
+                gain_sb[:, b : b + 1, :].to_broadcast([P, JB, 4]), ALU.mult)
+
+        def quantise_h(h_bf, b, pair):
+            jh, c0 = divmod(2 * JB * pair, 512)
+            nc.vector.quantize_mx(
+                h_codes[b][jh][:, c0 : c0 + 2 * JB].bitcast(FP8X4), h_plane[b][jh][:, c0 : c0 + 2 * JB],
+                h_bf[:].rearrange("p j t -> p (j t)"))
+
+        def scores(m, jh):
+            bank = psum.tile([P, 512], F32, name="bank", tag="bank")
+            for b in range(2):
+                nc.tensor.matmul_mx(
+                    bank[:], lhsT=v2_codes[b][:, P * m : P * (m + 1)].bitcast(FP8X4),
+                    lhsT_scale=v2_scale[4 * b : P, P * m : P * (m + 1)],
+                    rhs=h_codes[b][jh][:].bitcast(FP8X4), rhs_scale=h_plane[b][jh][:],
+                    start=(b == 0), stop=(b == 1))
+            return bank
+
+        for jb in range(8):
+            z_pass(z_banks[jb], 0, jb, 2)
+        waiting = None
+        for step in range(16):
+            b, jb = divmod(step, 8)
+            bank = z_banks[step]
+            s = silu(bank)
+            if jb % 2 == 0:
+                h_bf = ring.tile([P, 2 * JB, 4], BF16, name="h_bf", tag="h_bf", align_bytes=64)
+            scale(s, b, h_bf, jb % 2)
+            if waiting is not None:
+                quantise_h(*waiting)
+                waiting = None
+            if jb % 2 == 1:
+                waiting = (h_bf, b, jb // 2)
+            if b == 0:
+                z_banks.append(psum.tile([P, 512], F32, name="bank", tag="bank"))
+                z_pass(z_banks[8 + jb], 1, jb, 0)
+                z_pass(z_banks[8 + jb], 1, jb, 1)
+            if 4 <= step < 8:
+                z_pass(z_banks[2 * step], 1, 2 * step - 8, 2)
+                z_pass(z_banks[2 * step + 1], 1, 2 * step - 7, 2)
+            if step == 1:
+                round_w1(1, 2)
+            if step == 3:
+                quantise_w1(1)
+            if step in (6, 9):
+                b2 = 0 if step == 6 else 1
+                nc.vector.tensor_copy(v2_codes[b2][:], v2_win[b2][:].indirect(idx2[:]))
+            if step == 12:
+                for m in range(4):
+                    nc.scalar.copy(e_sb[m][:, 0:512], scores(m, 0)[:])
+        quantise_h(*waiting)
+
+        for m in range(4):
+            nc.vector.tensor_copy(e_sb[m][:, 512:1024], scores(m, 1)[:])
+        for m in range(4):
+            a_sb = ring.tile([P, NP], F32, name="a_sb", tag="a_sb")
+            nc.scalar.activation(a_sb[:], e_sb[m][:].indirect(p1[:]), ACT.Sigmoid, bias=tol_sb[:, m : m + 1])
+            al = ring.tile([P, NP], F32, name="al", tag="al")
+            nc.vector.tensor_tensor(al[:], a_sb[:], lean_sb[:, m, :], ALU.add)
+            res = ring.tile([P, NP], F32, name="res", tag="res")
+            nc.vector.tensor_tensor(res[:], e_sb[m][:].indirect(p2[:]), al[:], ALU.mult)
+            nc.sync.dma_start(out[P * m : P * (m + 1), :], res[:])

@@ -27,73 +27,93 @@ def tile_list_arbitrator_appointment_scores_kernel(
     nc = tc.nc
     with ExitStack() as ctx:
         keep = ctx.enter_context(tc.tile_pool(name="keep", bufs=1))
-        stage = ctx.enter_context(tc.tile_pool(name="stage", bufs=1))
         ring = ctx.enter_context(tc.tile_pool(name="ring", bufs=3))
         psum = ctx.enter_context(tc.psum_pool(name="psum", bufs=8))
 
         def held(name, shape, dtype):
             return keep.tile(shape, dtype, name=name, align_bytes=64)
 
-        def staged(name, shape, dtype, kib):
-            return stage.tile(shape, dtype, name=name, align_bytes=64, offset=1024 * kib)
-
         def words_of(table, a):
             return table[a].rearrange("p t i -> p (t i)").bitcast(I32)
+
+        def rows_of(scales):
+            return scales.rearrange("a q n -> q a n").bitcast(I32)
+
+        def spread(queue, plane, rows, first, passes):
+            for q in range(4):
+                r0 = first + 4 * passes * q
+                queue.dma_start(
+                    plane[32 * q : 32 * q + 4, :, :].bitcast(I32),
+                    rows[r0 : r0 + 4 * passes, :].bitcast(I32))
 
         idx = keep.tile([P, S // 16], U16, name="idx")
         idx2 = keep.tile([P, S2 // 16], U16, name="idx2")
         p1 = keep.tile([P, NP // 16], U16, name="p1")
         p2 = keep.tile([P, NP // 16], U16, name="p2")
 
-        v_scale_win = staged("v_scale_win", [P, T], U8, 40)
-        w4_scale_raw = staged("w4_scale_raw", [P, 2, H], U8, 48)
+        v_scale_win = held("v_scale_win", [P, T], U8)
+        w4_scale_raw = held("w4_scale_raw", [P, 2, H], U8)
         v2_scale_win = held("v2_scale_win", [P, T3], U8)
-        v_scale_1 = held("v_scale_1", [P, S], U8)
-        nc.vector.memset(v_scale_win[:].bitcast(I32), 0)
+        nc.gpsimd.memset(v_scale_win[:].bitcast(I32), 0)
         nc.vector.memset(w4_scale_raw[:].bitcast(I32), 0)
-        nc.vector.memset(v2_scale_win[:].bitcast(I32), 0)
-        nc.vector.memset(v_scale_1[:].bitcast(I32), 0)
+        for rows in (slice(32, 64), slice(64, P)):
+            nc.gpsimd.memset(v2_scale_win[rows, :].bitcast(I32), 0)
 
-        v_win = [staged("v_win%d" % a, [P, T], U32, 16 * (a % 2)) for a in range(3)]
-        v2_win = [staged("v2_win%d" % b, [P, T3], U32, 16 + 8 * b) for b in range(2)]
-        w1_raw = [staged("w1_raw%d" % b, [P, 4, 512], F32, 32 + 8 * b) for b in range(2)]
-        w4_raw = staged("w4_raw", [P, 2, H], U16, 30)
-        lean_sb = staged("lean_sb", [P, 4, NP], F32, 32)
-        gain_sb = staged("gain_sb", [P, 2, 4], F32, 48)
-        tol_sb = staged("tol_sb", [P, 4], F32, 49)
+        v_win = [held("v_win%d" % a, [P, T], U32) for a in range(3)]
+        v2_win = [held("v2_win%d" % b, [P, T3], U32) for b in range(2)]
+        w1_raw = [held("w1_raw%d" % b, [P, 4, 512], F32) for b in range(2)]
+        w4_raw = held("w4_raw", [P, 2, H], U16)
+        lean_sb = held("lean_sb", [P, 4, NP], F32)
+        gain_sb = held("gain_sb", [P, 2, 4], F32)
+        tol_sb = held("tol_sb", [P, 4], F32)
 
         def load_w1(b):
             nc.sync.dma_start(
                 w1_raw[b][:], w1[:, 512 * b : 512 * (b + 1)].rearrange("(p j) c -> p j c", j=4))
 
-        nc.sync.dma_start(idx[:], offs)
-        nc.sync.dma_start(idx2[:], offs2)
-        nc.sync.dma_start(p1[:], pos1)
-        nc.sync.dma_start(p2[:], pos2)
         nc.sync.dma_start(w4_raw[:].bitcast(I32), w4_words.rearrange("a p n -> p a n").bitcast(I32))
-        nc.sync.dma_start(v_win[0][:].bitcast(I32), words_of(tab_words, 0))
+        nc.sync.dma_start(idx[:], offs)
+        nc.sync.dma_start(gain_sb[:], gain.rearrange("(b p t) -> p b t", b=2, t=4))
+        load_w1(0)
+        nc.sync.dma_start(v_scale_win[0:32, :].bitcast(I32), rows_of(tab_scales[0:2]))
+        nc.sync.dma_start(v_scale_win[32:48, :].bitcast(I32), tab_scales[2].bitcast(I32))
         for q in range(4):
-            nc.scalar.dma_start(
-                v_scale_win[32 * q : 32 * q + 12, :].bitcast(I32),
-                tab_scales[:, 4 * q : 4 * q + 4, :].bitcast(I32))
-        for q in range(4):
-            (nc.scalar if q < 2 else nc.gpsimd).dma_start(
+            nc.sync.dma_start(
                 w4_scale_raw[32 * q : 32 * q + 4, :, :].bitcast(I32),
-                w4_scales[:, 4 * q : 4 * q + 4, :].rearrange("a r n -> r a n").bitcast(I32))
-        for q in range(4):
-            nc.gpsimd.dma_start(
-                v2_scale_win[32 * q : 32 * q + 8, :].bitcast(I32),
-                tab2_scales[:, 4 * q : 4 * q + 4, :].bitcast(I32))
+                rows_of(w4_scales[:, 4 * q : 4 * q + 4, :]))
+        nc.sync.dma_start(v_win[0][:].bitcast(I32), words_of(tab_words, 0))
+        nc.sync.dma_start(v2_scale_win[0:32, :].bitcast(I32), rows_of(tab2_scales))
+        nc.sync.dma_start(idx2[:], offs2)
 
         w4_codes = held("w4_codes", [P, 4, 4, P], U16)
-        w4_plane = held("w4_plane", [P, 4, 4, P], U8)
+        w4_plane = held("w4_plane", [P, 2, H], U8)
         nc.vector.tensor_copy(
-            w4_codes[:].rearrange("p g t q -> p g q t"),
-            w4_raw[:].rearrange("p a (b q t) -> p (a b) q t", b=2, t=4))
-        nc.sync.dma_start(v_win[1][:].bitcast(I32), words_of(tab_words, 1))
-        load_w1(0)
+            w4_codes[:], w4_raw[:].rearrange("p a (b q t) -> p (a b) t q", b=2, t=4))
 
-        v_scale = held("v_scale", [P, S], U8)
+        v_rows = held("v_rows", [P, S], U8)
+        v_plane01 = held("v_plane01", [P, 2, S], U8)
+        v_plane2 = held("v_plane2", [P, 1, S], U8)
+        nc.vector.tensor_copy(v_rows[:], v_scale_win[:].indirect(idx[:]))
+        spread(nc.sync, v_plane01, v_rows, 0, 2)
+
+        nc.vector.tensor_copy(
+            w4_plane[:].rearrange("p a (b t q) -> p (a b) t q", b=2, t=4),
+            w4_scale_raw[:].rearrange("p a (b q t) -> p (a b) t q", b=2, t=4))
+
+        nc.sync.dma_start(v_win[1][:].bitcast(I32), words_of(tab_words, 1))
+        spread(nc.sync, v_plane2, v_rows, 32, 1)
+        nc.sync.dma_start(v_win[2][:].bitcast(I32), words_of(tab_words, 2))
+        load_w1(1)
+        for b in range(2):
+            nc.sync.dma_start(v2_win[b][:].bitcast(I32), words_of(tab2_words, b))
+        nc.sync.dma_start(p1[:], pos1)
+        nc.sync.dma_start(p2[:], pos2)
+        with nc.allow_non_contiguous_dma(reason="one value of tol for each partition"):
+            nc.sync.dma_start(tol_sb[:], tol.rearrange("(m p) -> p m", m=4))
+        nc.sync.dma_start(lean_sb[:], lean.rearrange("(m p) n -> p m n", m=4))
+
+        v2_rows = held("v2_rows", [P, S2], U8)
+        v2_plane = held("v2_plane", [P, 2, S2], U8)
 
         v_codes = [held("v_codes%d" % a, [P, S], U32) for a in range(3)]
 
@@ -107,12 +127,10 @@ def tile_list_arbitrator_appointment_scores_kernel(
         w1_codes = [held("w1_codes%d" % b, [P, 512], U32) for b in range(2)]
         w1_plane = [held("w1_plane%d" % b, [P, 512], U8) for b in range(2)]
 
-        def round_w1(b, halves):
-            width = P // halves
-            for m0 in range(0, P, width):
-                nc.scalar.copy(
-                    w1_bf[b][:, :, m0 : m0 + width, :].rearrange("p t m j -> p m j t"),
-                    w1_raw[b][:, :, 4 * m0 : 4 * (m0 + width)].rearrange("p j (m t) -> p m j t", t=4))
+        def round_w1(b, m0, m1):
+            nc.scalar.copy(
+                w1_bf[b][:, :, m0:m1, :].rearrange("p t m j -> p m j t"),
+                w1_raw[b][:, :, 4 * m0 : 4 * m1].rearrange("p j (m t) -> p m j t", t=4))
 
         def quantise_w1(b):
             nc.vector.quantize_mx(
@@ -120,50 +138,32 @@ def tile_list_arbitrator_appointment_scores_kernel(
                 w1_bf[b][:].rearrange("p t m j -> p (t m j)"))
 
         v2_codes = [held("v2_codes%d" % b, [P, S2], U32) for b in range(2)]
-        v2_scale = held("v2_scale", [P, S2], U8)
 
         def z_pass(bank, b, jb, a):
             cols = slice(JB * jb, JB * (jb + 1))
             for t in range(4):
                 if a < 2:
                     lhsT = w4_codes[:, 2 * a + b, t, :].bitcast(FP4X4)
-                    lhsT_scale = w4_plane[:, 2 * a + b, t, :]
-                    rhs_scale = (v_scale if a == 0 else v_scale_1)[:, cols]
+                    lhsT_scale = w4_plane[:, a, 512 * b + P * t : 512 * b + P * (t + 1)]
                 else:
                     lhsT = w1_codes[b][:, P * t : P * (t + 1)].bitcast(FP8X4)
                     lhsT_scale = w1_plane[b][:, P * t : P * (t + 1)]
-                    rhs_scale = v_scale[8:P, cols]
                 nc.tensor.matmul_mx(
                     bank[:, JB * t : JB * (t + 1)], lhsT=lhsT, lhsT_scale=lhsT_scale,
-                    rhs=v_codes[a][:, cols].bitcast(FP8X4), rhs_scale=rhs_scale,
+                    rhs=v_codes[a][:, cols].bitcast(FP8X4), rhs_scale=v_plane01[:, a, cols] if a < 2 else v_plane2[:, 0, cols],
                     start=(a == 0 and t == 0), stop=(a == 2 and t == 3))
 
+        round_w1(0, 0, P)
+        quantise_w1(0)
         gather_v(0, 512)
-        nc.sync.dma_start(v_win[2][:].bitcast(I32), words_of(tab_words, 2))
-        nc.vector.tensor_copy(v_scale[:], v_scale_win[:].indirect(idx[:]))
-        nc.scalar.dma_start(v_scale_1[0:100, :].bitcast(I32), v_scale[4:104, :].bitcast(I32))
-        load_w1(1)
-
-        nc.vector.tensor_copy(
-            w4_plane[:].rearrange("p g t q -> p g q t"),
-            w4_scale_raw[:].rearrange("p a (b q t) -> p (a b) q t", b=2, t=4))
-        nc.sync.dma_start(gain_sb[:], gain.rearrange("(b p t) -> p b t", b=2, t=4))
-        with nc.allow_non_contiguous_dma(reason="one value of tol for each partition"):
-            nc.sync.dma_start(tol_sb[:], tol.rearrange("(m p) -> p m", m=4))
-
-
         z_banks = [psum.tile([P, 512], F32, name="bank", tag="bank") for jb in range(8)]
         for jb in range(8):
             z_pass(z_banks[jb], 0, jb, 0)
+        nc.vector.tensor_copy(v2_rows[:], v2_scale_win[:].indirect(idx2[:]))
+        spread(nc.gpsimd, v2_plane, v2_rows, 0, 2)
         gather_v(1, 512)
-        for b in range(2):
-            nc.sync.dma_start(v2_win[b][:].bitcast(I32), words_of(tab2_words, b))
         for jb in range(8):
             z_pass(z_banks[jb], 0, jb, 1)
-        nc.vector.tensor_copy(v2_scale[:], v2_scale_win[:].indirect(idx2[:]))
-        round_w1(0, 1)
-        nc.sync.dma_start(lean_sb[:], lean.rearrange("(m p) n -> p m n", m=4))
-        quantise_w1(0)
         gather_v(2, 256)
 
         h_codes = [[held("h_codes%d%d" % (b, jh), [P, 512], U32) for jh in range(2)] for b in range(2)]
@@ -186,23 +186,20 @@ def tile_list_arbitrator_appointment_scores_kernel(
                 h_codes[b][jh][:, c0 : c0 + 2 * JB].bitcast(FP8X4), h_plane[b][jh][:, c0 : c0 + 2 * JB],
                 h_bf[:].rearrange("p j t -> p (j t)"))
 
-        def scores(m, jh):
-            bank = psum.tile([P, 512], F32, name="bank", tag="bank")
-            for b in range(2):
-                nc.tensor.matmul_mx(
-                    bank[:], lhsT=v2_codes[b][:, P * m : P * (m + 1)].bitcast(FP8X4),
-                    lhsT_scale=v2_scale[4 * b : P, P * m : P * (m + 1)],
-                    rhs=h_codes[b][jh][:].bitcast(FP8X4), rhs_scale=h_plane[b][jh][:],
-                    start=(b == 0), stop=(b == 1))
-            return bank
+        def score_pass(bank, m, jh, b):
+            nc.tensor.matmul_mx(
+                bank[:], lhsT=v2_codes[b][:, P * m : P * (m + 1)].bitcast(FP8X4),
+                lhsT_scale=v2_plane[:, b, P * m : P * (m + 1)],
+                rhs=h_codes[b][jh][:].bitcast(FP8X4), rhs_scale=h_plane[b][jh][:],
+                start=(b == 0), stop=(b == 1))
 
         for jb in range(8):
             z_pass(z_banks[jb], 0, jb, 2)
         waiting = None
+        last = []
         for step in range(16):
             b, jb = divmod(step, 8)
-            bank = z_banks[step]
-            s = silu(bank)
+            s = silu(z_banks[step])
             if jb % 2 == 0:
                 h_bf = ring.tile([P, 2 * JB, 4], BF16, name="h_bf", tag="h_bf", align_bytes=64)
             scale(s, b, h_bf, jb % 2)
@@ -215,28 +212,42 @@ def tile_list_arbitrator_appointment_scores_kernel(
                 z_banks.append(psum.tile([P, 512], F32, name="bank", tag="bank"))
                 z_pass(z_banks[8 + jb], 1, jb, 0)
                 z_pass(z_banks[8 + jb], 1, jb, 1)
+            if step < 4:
+                round_w1(1, 32 * step, 32 * (step + 1))
+            if step == 4:
+                quantise_w1(1)
             if 4 <= step < 8:
                 z_pass(z_banks[2 * step], 1, 2 * step - 8, 2)
                 z_pass(z_banks[2 * step + 1], 1, 2 * step - 7, 2)
-            if step == 1:
-                round_w1(1, 2)
-            if step == 3:
-                quantise_w1(1)
             if step in (6, 9):
                 b2 = 0 if step == 6 else 1
                 nc.vector.tensor_copy(v2_codes[b2][:], v2_win[b2][:].indirect(idx2[:]))
             if step == 12:
                 for m in range(4):
-                    nc.scalar.copy(e_sb[m][:, 0:512], scores(m, 0)[:])
+                    bank = psum.tile([P, 512], F32, name="bank", tag="bank")
+                    score_pass(bank, m, 0, 0)
+                    score_pass(bank, m, 0, 1)
+                    nc.scalar.copy(e_sb[m][:, 0:512], bank[:])
+            if step >= 12:
+                last.append(psum.tile([P, 512], F32, name="bank", tag="bank"))
+                score_pass(last[-1], step - 12, 1, 0)
         quantise_h(*waiting)
 
         for m in range(4):
-            nc.vector.tensor_copy(e_sb[m][:, 512:1024], scores(m, 1)[:])
-        for m in range(4):
-            a_sb = ring.tile([P, NP], F32, name="a_sb", tag="a_sb")
-            nc.scalar.activation(a_sb[:], e_sb[m][:].indirect(p1[:]), ACT.Sigmoid, bias=tol_sb[:, m : m + 1])
-            al = ring.tile([P, NP], F32, name="al", tag="al")
-            nc.vector.tensor_tensor(al[:], a_sb[:], lean_sb[:, m, :], ALU.add)
-            res = ring.tile([P, NP], F32, name="res", tag="res")
-            nc.vector.tensor_tensor(res[:], e_sb[m][:].indirect(p2[:]), al[:], ALU.mult)
-            nc.sync.dma_start(out[P * m : P * (m + 1), :], res[:])
+            score_pass(last[m], m, 1, 1)
+        nc.vector.tensor_copy(e_sb[0][:, 512:1024], last[0][:])
+        picked = held("picked", [P, NP], F32)
+        nc.vector.tensor_copy(picked[:], e_sb[0][:].indirect(p2[:]))
+        nc.vector.tensor_copy(e_sb[1][:, 512:1024], last[1][:])
+        for m, c0, c1 in ((0, 0, NP), (1, 0, NP), (2, 0, NP), (3, 0, NP // 2), (3, NP // 2, NP)):
+            a_sb = ring.tile([P, c1 - c0], F32, name="a_sb", tag="a_sb")
+            nc.scalar.activation(
+                a_sb[:], e_sb[m][:].indirect(p1[:, c0 // 16 : c1 // 16]), ACT.Sigmoid, bias=tol_sb[:, m : m + 1])
+            if m < 2:
+                nc.scalar.copy(e_sb[m + 2][:, 512:1024], last[m + 2][:])
+            al = ring.tile([P, c1 - c0], F32, name="al", tag="al")
+            nc.vector.tensor_tensor(al[:], a_sb[:], lean_sb[:, m, c0:c1], ALU.add)
+            res = ring.tile([P, c1 - c0], F32, name="res", tag="res")
+            scores = picked[:] if m == 0 else e_sb[m][:].indirect(p2[:, c0 // 16 : c1 // 16])
+            nc.vector.tensor_tensor(res[:], scores, al[:], ALU.mult)
+            nc.sync.dma_start(out[P * m : P * (m + 1), c0:c1], res[:])

@@ -17,6 +17,7 @@ ACT = mybir.ActivationFunctionType
 ALU = mybir.AluOpType
 
 P = 128
+HALF = NP // 2
 JB = 128
 
 
@@ -140,8 +141,9 @@ def tile_list_arbitrator_appointment_scores_kernel(
         v2_codes = [held("v2_codes%d" % b, [P, S2], U32) for b in range(2)]
 
         def z_pass(bank, b, jb, a):
-            cols = slice(JB * jb, JB * (jb + 1))
-            for t in range(4):
+            jq, u = divmod(jb, 2)
+            cols = slice(2 * JB * jq, 2 * JB * (jq + 1))
+            for t in (2 * u, 2 * u + 1):
                 if a < 2:
                     lhsT = w4_codes[:, 2 * a + b, t, :].bitcast(FP4X4)
                     lhsT_scale = w4_plane[:, a, 512 * b + P * t : 512 * b + P * (t + 1)]
@@ -149,9 +151,9 @@ def tile_list_arbitrator_appointment_scores_kernel(
                     lhsT = w1_codes[b][:, P * t : P * (t + 1)].bitcast(FP8X4)
                     lhsT_scale = w1_plane[b][:, P * t : P * (t + 1)]
                 nc.tensor.matmul_mx(
-                    bank[:, JB * t : JB * (t + 1)], lhsT=lhsT, lhsT_scale=lhsT_scale,
+                    bank[:, 2 * JB * (t % 2) : 2 * JB * (t % 2 + 1)], lhsT=lhsT, lhsT_scale=lhsT_scale,
                     rhs=v_codes[a][:, cols].bitcast(FP8X4), rhs_scale=v_plane01[:, a, cols] if a < 2 else v_plane2[:, 0, cols],
-                    start=(a == 0 and t == 0), stop=(a == 2 and t == 3))
+                    start=(a == 0 and t % 2 == 0), stop=(a == 2 and t % 2 == 1))
 
         round_w1(0, 0, P)
         quantise_w1(0)
@@ -170,15 +172,16 @@ def tile_list_arbitrator_appointment_scores_kernel(
         h_plane = [[held("h_plane%d%d" % (b, jh), [P, 512], U8) for jh in range(2)] for b in range(2)]
         e_sb = [held("e_sb%d" % m, [P, S], F32) for m in range(4)]
 
-        def silu(bank):
-            s = ring.tile([P, JB, 4], F32, name="silu", tag="silu")
-            nc.scalar.activation(s[:], bank[:].rearrange("p (t j) -> p j t", t=4), ACT.Silu)
-            return s
+        def silu(bank, s, half):
+            nc.scalar.activation(
+                s[:, half, :, :], bank[:].rearrange("p (t j) -> p j t", t=2), ACT.Silu)
 
-        def scale(s, b, h_bf, half):
+        def scale(s, b, h_bf, c0, c1):
             nc.vector.tensor_tensor(
-                h_bf[:, JB * half : JB * (half + 1), :], s[:],
-                gain_sb[:, b : b + 1, :].to_broadcast([P, JB, 4]), ALU.mult)
+                h_bf[:, c0:c1, :].rearrange("p j (u t) -> p j u t", u=2),
+                s[:, :, c0:c1, :].rearrange("p u j t -> p j u t"),
+                gain_sb[:, b : b + 1, :].to_broadcast([P, c1 - c0, 4]).rearrange("p j (u t) -> p j u t", u=2),
+                ALU.mult)
 
         def quantise_h(h_bf, b, pair):
             jh, c0 = divmod(2 * JB * pair, 512)
@@ -196,18 +199,23 @@ def tile_list_arbitrator_appointment_scores_kernel(
         for jb in range(8):
             z_pass(z_banks[jb], 0, jb, 2)
         waiting = None
-        last = []
+        first, last = [], []
         for step in range(16):
             b, jb = divmod(step, 8)
-            s = silu(z_banks[step])
             if jb % 2 == 0:
+                s = ring.tile([P, 2, 2 * JB, 2], F32, name="silu", tag="silu")
                 h_bf = ring.tile([P, 2 * JB, 4], BF16, name="h_bf", tag="h_bf", align_bytes=64)
-            scale(s, b, h_bf, jb % 2)
-            if waiting is not None:
+            silu(z_banks[step], s, jb % 2)
+            if jb % 2 == 1:
+                scale(s, b, h_bf, 0, 2 * JB)
+            if waiting is not None and (jb % 2 == 1 or step == 14):
                 quantise_h(*waiting)
                 waiting = None
             if jb % 2 == 1:
                 waiting = (h_bf, b, jb // 2)
+            if step == 15:
+                warm = held("warm", [P, 1], F32)
+                nc.scalar.activation(warm[:], s[:, 1, 0, 0:1], ACT.Sigmoid)
             if b == 0:
                 z_banks.append(psum.tile([P, 512], F32, name="bank", tag="bank"))
                 z_pass(z_banks[8 + jb], 1, jb, 0)
@@ -222,32 +230,50 @@ def tile_list_arbitrator_appointment_scores_kernel(
             if step in (6, 9):
                 b2 = 0 if step == 6 else 1
                 nc.vector.tensor_copy(v2_codes[b2][:], v2_win[b2][:].indirect(idx2[:]))
-            if step == 12:
+            if step == 11:
+                quantise_h(*waiting)
+                waiting = None
                 for m in range(4):
-                    bank = psum.tile([P, 512], F32, name="bank", tag="bank")
-                    score_pass(bank, m, 0, 0)
-                    score_pass(bank, m, 0, 1)
-                    nc.scalar.copy(e_sb[m][:, 0:512], bank[:])
+                    first.append(psum.tile([P, 512], F32, name="bank", tag="bank"))
+                    score_pass(first[m], m, 0, 0)
+                    score_pass(first[m], m, 0, 1)
             if step >= 12:
                 last.append(psum.tile([P, 512], F32, name="bank", tag="bank"))
                 score_pass(last[-1], step - 12, 1, 0)
         quantise_h(*waiting)
 
         for m in range(4):
+            nc.scalar.copy(e_sb[m][:, 0:512], first[m][:])
+        for m in range(4):
             score_pass(last[m], m, 1, 1)
-        nc.vector.tensor_copy(e_sb[0][:, 512:1024], last[0][:])
-        picked = held("picked", [P, NP], F32)
-        nc.vector.tensor_copy(picked[:], e_sb[0][:].indirect(p2[:]))
-        nc.vector.tensor_copy(e_sb[1][:, 512:1024], last[1][:])
-        for m, c0, c1 in ((0, 0, NP), (1, 0, NP), (2, 0, NP), (3, 0, NP // 2), (3, NP // 2, NP)):
-            a_sb = ring.tile([P, c1 - c0], F32, name="a_sb", tag="a_sb")
+        for m in range(2):
+            nc.vector.tensor_copy(e_sb[m][:, 512:1024], last[m][:])
+
+        res = [held("res%d" % m, [P, NP], F32) for m in range(4)]
+
+        def look(m, cols, entries):
+            a_sb = ring.tile([P, HALF], F32, name="a_sb", tag="a_sb", bufs=4)
             nc.scalar.activation(
-                a_sb[:], e_sb[m][:].indirect(p1[:, c0 // 16 : c1 // 16]), ACT.Sigmoid, bias=tol_sb[:, m : m + 1])
+                a_sb[:], e_sb[m][:].indirect(p1[:, entries]), ACT.Sigmoid, bias=tol_sb[:, m : m + 1])
+            al = ring.tile([P, HALF], F32, name="al", tag="al")
+            nc.vector.tensor_tensor(al[:], a_sb[:], lean_sb[:, m, cols], ALU.add)
+            return al
+
+        def finish(m, cols, entries, al):
+            nc.vector.tensor_tensor(res[m][:, cols], e_sb[m][:].indirect(p2[:, entries]), al[:], ALU.mult)
+            if m == 3:
+                nc.sync.dma_start(out[P * m : P * (m + 1), cols], res[m][:, cols])
+            elif cols.stop == NP:
+                nc.sync.dma_start(out[P * m : P * (m + 1), :], res[m][:])
+
+        waiting = None
+        for m in range(4):
+            for c0 in (0, HALF):
+                cols, entries = slice(c0, c0 + HALF), slice(c0 // 16, (c0 + HALF) // 16)
+                al = look(m, cols, entries)
+                if waiting is not None:
+                    finish(*waiting)
+                waiting = (m, cols, entries, al)
             if m < 2:
                 nc.scalar.copy(e_sb[m + 2][:, 512:1024], last[m + 2][:])
-            al = ring.tile([P, c1 - c0], F32, name="al", tag="al")
-            nc.vector.tensor_tensor(al[:], a_sb[:], lean_sb[:, m, c0:c1], ALU.add)
-            res = ring.tile([P, c1 - c0], F32, name="res", tag="res")
-            scores = picked[:] if m == 0 else e_sb[m][:].indirect(p2[:, c0 // 16 : c1 // 16])
-            nc.vector.tensor_tensor(res[:], scores, al[:], ALU.mult)
-            nc.sync.dma_start(out[P * m : P * (m + 1), c0:c1], res[:])
+        finish(*waiting)

@@ -208,7 +208,7 @@ def tile_list_arbitrator_appointment_scores_kernel(
             silu(z_banks[step], s, jb % 2)
             if jb % 2 == 1:
                 scale(s, b, h_bf, 0, 2 * JB)
-            if waiting is not None and (jb % 2 == 1 or step == 14):
+            if waiting is not None and jb % 2 == 1:
                 quantise_h(*waiting)
                 waiting = None
             if jb % 2 == 1:
@@ -220,15 +220,18 @@ def tile_list_arbitrator_appointment_scores_kernel(
                 z_banks.append(psum.tile([P, 512], F32, name="bank", tag="bank"))
                 z_pass(z_banks[8 + jb], 1, jb, 0)
                 z_pass(z_banks[8 + jb], 1, jb, 1)
-            if step < 4:
-                round_w1(1, 32 * step, 32 * (step + 1))
-            if step == 4:
+            if step in (3, 5):
+                m0 = 0 if step == 3 else 64
+                round_w1(1, m0, m0 + 32)
+                round_w1(1, m0 + 32, m0 + 64)
+            if step == 5:
                 quantise_w1(1)
-            if 4 <= step < 8:
-                z_pass(z_banks[2 * step], 1, 2 * step - 8, 2)
-                z_pass(z_banks[2 * step + 1], 1, 2 * step - 7, 2)
-            if step in (6, 9):
-                b2 = 0 if step == 6 else 1
+                for early in range(5):
+                    z_pass(z_banks[8 + early], 1, early, 2)
+            if 5 <= step < 8:
+                z_pass(z_banks[8 + jb], 1, jb, 2)
+            if step in (3, 7):
+                b2 = 0 if step == 3 else 1
                 nc.vector.tensor_copy(v2_codes[b2][:], v2_win[b2][:].indirect(idx2[:]))
             if step == 11:
                 quantise_h(*waiting)

from contextlib import ExitStack

import concourse.mybir as mybir

K, K4, K1, H, T, S, T3, S2, NP = 1536, 1024, 512, 1024, 4096, 1024, 2048, 512, 512
FLOPS = 2 * K * H * S + 2 * H * S2 * S

F32 = mybir.dt.float32
BF16 = mybir.dt.bfloat16
I32 = mybir.dt.int32
U32 = mybir.dt.uint32
U16 = mybir.dt.uint16
U8 = mybir.dt.uint8
FP8X4 = mybir.dt.float8_e4m3fn_x4
FP4X4 = mybir.dt.float4_e2m1fn_x4
ACT = mybir.ActivationFunctionType
ALU = mybir.AluOpType

P = 128
HALF = NP // 2
JB = 128


def tile_list_arbitrator_appointment_scores_kernel(
    tc, tab_words, tab_scales, tab2_words, tab2_scales, offs, offs2, pos1, pos2,
    w4_words, w4_scales, w1, gain, tol, lean, out,
):
    nc = tc.nc
    with ExitStack() as ctx:
        keep = ctx.enter_context(tc.tile_pool(name="keep", bufs=1))
        ring = ctx.enter_context(tc.tile_pool(name="ring", bufs=3))
        psum = ctx.enter_context(tc.psum_pool(name="psum", bufs=8))

        def held(name, shape, dtype):
            return keep.tile(shape, dtype, name=name, align_bytes=64)

        def words_of(table, a):
            return table[a].rearrange("p t i -> p (t i)").bitcast(I32)

        def rows_of(scales):
            return scales.rearrange("a q n -> q a n").bitcast(I32)

        def spread(queue, plane, rows, first, passes):
            for q in range(4):
                r0 = first + 4 * passes * q
                queue.dma_start(
                    plane[32 * q : 32 * q + 4, :, :].bitcast(I32),
                    rows[r0 : r0 + 4 * passes, :].bitcast(I32))

        idx = keep.tile([P, S // 16], U16, name="idx")
        idx2 = keep.tile([P, S2 // 16], U16, name="idx2")
        p1 = keep.tile([P, NP // 16], U16, name="p1")
        p2 = keep.tile([P, NP // 16], U16, name="p2")

        v_scale_win = held("v_scale_win", [P, T], U8)
        w4_scale_raw = held("w4_scale_raw", [P, 2, H], U8)
        v2_scale_win = held("v2_scale_win", [P, T3], U8)
        nc.gpsimd.memset(v_scale_win[:].bitcast(I32), 0)
        nc.vector.memset(w4_scale_raw[:].bitcast(I32), 0)
        for rows in (slice(32, 64), slice(64, P)):
            nc.gpsimd.memset(v2_scale_win[rows, :].bitcast(I32), 0)

        v_win = [held("v_win%d" % a, [P, T], U32) for a in range(3)]
        v2_win = [held("v2_win%d" % b, [P, T3], U32) for b in range(2)]
        w1_raw = [held("w1_raw%d" % b, [P, 4, 512], F32) for b in range(2)]
        w4_raw = held("w4_raw", [P, 2, H], U16)
        lean_sb = held("lean_sb", [P, 4, NP], F32)
        gain_sb = held("gain_sb", [P, 2, 4], F32)
        tol_sb = held("tol_sb", [P, 4], F32)

        def load_w1(b):
            nc.sync.dma_start(
                w1_raw[b][:], w1[:, 512 * b : 512 * (b + 1)].rearrange("(p j) c -> p j c", j=4))

        nc.sync.dma_start(w4_raw[:].bitcast(I32), w4_words.rearrange("a p n -> p a n").bitcast(I32))
        nc.sync.dma_start(idx[:], offs)
        nc.sync.dma_start(gain_sb[:], gain.rearrange("(b p t) -> p b t", b=2, t=4))
        load_w1(0)
        nc.sync.dma_start(v_scale_win[0:32, :].bitcast(I32), rows_of(tab_scales[0:2]))
        nc.sync.dma_start(v_scale_win[32:48, :].bitcast(I32), tab_scales[2].bitcast(I32))
        for q in range(4):
            nc.sync.dma_start(
                w4_scale_raw[32 * q : 32 * q + 4, :, :].bitcast(I32),
                rows_of(w4_scales[:, 4 * q : 4 * q + 4, :]))
        nc.sync.dma_start(v_win[0][:].bitcast(I32), words_of(tab_words, 0))
        nc.sync.dma_start(v2_scale_win[0:32, :].bitcast(I32), rows_of(tab2_scales))
        nc.sync.dma_start(idx2[:], offs2)

        w4_codes = held("w4_codes", [P, 4, 4, P], U16)
        w4_plane = held("w4_plane", [P, 2, H], U8)
        nc.vector.tensor_copy(
            w4_codes[:], w4_raw[:].rearrange("p a (b q t) -> p (a b) t q", b=2, t=4))

        v_rows = held("v_rows", [P, S], U8)
        v_plane01 = held("v_plane01", [P, 2, S], U8)
        v_plane2 = held("v_plane2", [P, 1, S], U8)
        nc.vector.tensor_copy(v_rows[:], v_scale_win[:].indirect(idx[:]))
        spread(nc.sync, v_plane01, v_rows, 0, 2)

        nc.vector.tensor_copy(
            w4_plane[:].rearrange("p a (b t q) -> p (a b) t q", b=2, t=4),
            w4_scale_raw[:].rearrange("p a (b q t) -> p (a b) t q", b=2, t=4))

        nc.sync.dma_start(v_win[1][:].bitcast(I32), words_of(tab_words, 1))
        spread(nc.sync, v_plane2, v_rows, 32, 1)
        nc.sync.dma_start(v_win[2][:].bitcast(I32), words_of(tab_words, 2))
        load_w1(1)
        for b in range(2):
            nc.sync.dma_start(v2_win[b][:].bitcast(I32), words_of(tab2_words, b))
        nc.sync.dma_start(p1[:], pos1)
        nc.sync.dma_start(p2[:], pos2)
        with nc.allow_non_contiguous_dma(reason="one value of tol for each partition"):
            nc.sync.dma_start(tol_sb[:], tol.rearrange("(m p) -> p m", m=4))
        nc.sync.dma_start(lean_sb[:], lean.rearrange("(m p) n -> p m n", m=4))

        v2_rows = held("v2_rows", [P, S2], U8)
        v2_plane = held("v2_plane", [P, 2, S2], U8)

        v_codes = [held("v_codes%d" % a, [P, S], U32) for a in range(3)]

        def gather_v(a, width):
            for c0 in range(0, S, width):
                nc.vector.tensor_copy(
                    v_codes[a][:, c0 : c0 + width],
                    v_win[a][:].indirect(idx[:, c0 // 16 : (c0 + width) // 16]))

        w1_bf = [held("w1_bf%d" % b, [P, 4, P, 4], BF16) for b in range(2)]
        w1_codes = [held("w1_codes%d" % b, [P, 512], U32) for b in range(2)]
        w1_plane = [held("w1_plane%d" % b, [P, 512], U8) for b in range(2)]

        def round_w1(b, m0, m1):
            nc.scalar.copy(
                w1_bf[b][:, :, m0:m1, :].rearrange("p t m j -> p m j t"),
                w1_raw[b][:, :, 4 * m0 : 4 * m1].rearrange("p j (m t) -> p m j t", t=4))

        def quantise_w1(b):
            nc.vector.quantize_mx(
                w1_codes[b][:].bitcast(FP8X4), w1_plane[b][:],
                w1_bf[b][:].rearrange("p t m j -> p (t m j)"))

        v2_codes = [held("v2_codes%d" % b, [P, S2], U32) for b in range(2)]

        def z_pass(bank, b, jb, a):
            jq, u = divmod(jb, 2)
            cols = slice(2 * JB * jq, 2 * JB * (jq + 1))
            for t in (2 * u, 2 * u + 1):
                if a < 2:
                    lhsT = w4_codes[:, 2 * a + b, t, :].bitcast(FP4X4)
                    lhsT_scale = w4_plane[:, a, 512 * b + P * t : 512 * b + P * (t + 1)]
                else:
                    lhsT = w1_codes[b][:, P * t : P * (t + 1)].bitcast(FP8X4)
                    lhsT_scale = w1_plane[b][:, P * t : P * (t + 1)]
                nc.tensor.matmul_mx(
                    bank[:, 2 * JB * (t % 2) : 2 * JB * (t % 2 + 1)], lhsT=lhsT, lhsT_scale=lhsT_scale,
                    rhs=v_codes[a][:, cols].bitcast(FP8X4), rhs_scale=v_plane01[:, a, cols] if a < 2 else v_plane2[:, 0, cols],
                    start=(a == 0 and t % 2 == 0), stop=(a == 2 and t % 2 == 1))

        round_w1(0, 0, P)
        quantise_w1(0)
        gather_v(0, 512)
        z_banks = [psum.tile([P, 512], F32, name="bank", tag="bank") for jb in range(8)]
        for jb in range(8):
            z_pass(z_banks[jb], 0, jb, 0)
        nc.vector.tensor_copy(v2_rows[:], v2_scale_win[:].indirect(idx2[:]))
        spread(nc.gpsimd, v2_plane, v2_rows, 0, 2)
        gather_v(1, 512)
        for jb in range(8):
            z_pass(z_banks[jb], 0, jb, 1)
        gather_v(2, 256)

        h_codes = [[held("h_codes%d%d" % (b, jh), [P, 512], U32) for jh in range(2)] for b in range(2)]
        h_plane = [[held("h_plane%d%d" % (b, jh), [P, 512], U8) for jh in range(2)] for b in range(2)]
        e_sb = [held("e_sb%d" % m, [P, S], F32) for m in range(4)]

        def silu(bank, s, half):
            nc.scalar.activation(
                s[:, half, :, :], bank[:].rearrange("p (t j) -> p j t", t=2), ACT.Silu)

        def scale(s, b, h_bf, c0, c1):
            nc.vector.tensor_tensor(
                h_bf[:, c0:c1, :].rearrange("p j (u t) -> p j u t", u=2),
                s[:, :, c0:c1, :].rearrange("p u j t -> p j u t"),
                gain_sb[:, b : b + 1, :].to_broadcast([P, c1 - c0, 4]).rearrange("p j (u t) -> p j u t", u=2),
                ALU.mult)

        def quantise_h(h_bf, b, pair):
            jh, c0 = divmod(2 * JB * pair, 512)
            nc.vector.quantize_mx(
                h_codes[b][jh][:, c0 : c0 + 2 * JB].bitcast(FP8X4), h_plane[b][jh][:, c0 : c0 + 2 * JB],
                h_bf[:].rearrange("p j t -> p (j t)"))

        def score_pass(bank, m, jh, b):
            nc.tensor.matmul_mx(
                bank[:], lhsT=v2_codes[b][:, P * m : P * (m + 1)].bitcast(FP8X4),
                lhsT_scale=v2_plane[:, b, P * m : P * (m + 1)],
                rhs=h_codes[b][jh][:].bitcast(FP8X4), rhs_scale=h_plane[b][jh][:],
                start=(b == 0), stop=(b == 1))

        for jb in range(8):
            z_pass(z_banks[jb], 0, jb, 2)
        waiting = None
        first, last = [], []
        for step in range(16):
            b, jb = divmod(step, 8)
            if jb % 2 == 0:
                s = ring.tile([P, 2, 2 * JB, 2], F32, name="silu", tag="silu")
                h_bf = ring.tile([P, 2 * JB, 4], BF16, name="h_bf", tag="h_bf", align_bytes=64)
            silu(z_banks[step], s, jb % 2)
            if jb % 2 == 1:
                scale(s, b, h_bf, 0, 2 * JB)
            if waiting is not None and jb % 2 == 1:
                quantise_h(*waiting)
                waiting = None
            if jb % 2 == 1:
                waiting = (h_bf, b, jb // 2)
            if step == 15:
                warm = held("warm", [P, 1], F32)
                nc.scalar.activation(warm[:], s[:, 1, 0, 0:1], ACT.Sigmoid)
            if b == 0:
                z_banks.append(psum.tile([P, 512], F32, name="bank", tag="bank"))
                z_pass(z_banks[8 + jb], 1, jb, 0)
                z_pass(z_banks[8 + jb], 1, jb, 1)
            if step in (3, 5):
                m0 = 0 if step == 3 else 64
                round_w1(1, m0, m0 + 32)
                round_w1(1, m0 + 32, m0 + 64)
            if step == 5:
                quantise_w1(1)
                for early in range(5):
                    z_pass(z_banks[8 + early], 1, early, 2)
            if 5 <= step < 8:
                z_pass(z_banks[8 + jb], 1, jb, 2)
            if step in (3, 7):
                b2 = 0 if step == 3 else 1
                nc.vector.tensor_copy(v2_codes[b2][:], v2_win[b2][:].indirect(idx2[:]))
            if step == 11:
                quantise_h(*waiting)
                waiting = None
                for m in range(4):
                    first.append(psum.tile([P, 512], F32, name="bank", tag="bank"))
                    score_pass(first[m], m, 0, 0)
                    score_pass(first[m], m, 0, 1)
            if step >= 12:
                last.append(psum.tile([P, 512], F32, name="bank", tag="bank"))
                score_pass(last[-1], step - 12, 1, 0)
        quantise_h(*waiting)

        for m in range(4):
            nc.scalar.copy(e_sb[m][:, 0:512], first[m][:])
        for m in range(4):
            score_pass(last[m], m, 1, 1)
        for m in range(2):
            nc.vector.tensor_copy(e_sb[m][:, 512:1024], last[m][:])

        res = [held("res%d" % m, [P, NP], F32) for m in range(4)]

        def look(m, cols, entries):
            a_sb = ring.tile([P, HALF], F32, name="a_sb", tag="a_sb", bufs=4)
            nc.scalar.activation(
                a_sb[:], e_sb[m][:].indirect(p1[:, entries]), ACT.Sigmoid, bias=tol_sb[:, m : m + 1])
            al = ring.tile([P, HALF], F32, name="al", tag="al")
            nc.vector.tensor_tensor(al[:], a_sb[:], lean_sb[:, m, cols], ALU.add)
            return al

        def finish(m, cols, entries, al):
            nc.vector.tensor_tensor(res[m][:, cols], e_sb[m][:].indirect(p2[:, entries]), al[:], ALU.mult)
            if m == 3:
                nc.sync.dma_start(out[P * m : P * (m + 1), cols], res[m][:, cols])
            elif cols.stop == NP:
                nc.sync.dma_start(out[P * m : P * (m + 1), :], res[m][:])

        waiting = None
        for m in range(4):
            for c0 in (0, HALF):
                cols, entries = slice(c0, c0 + HALF), slice(c0 // 16, (c0 + HALF) // 16)
                al = look(m, cols, entries)
                if waiting is not None:
                    finish(*waiting)
                waiting = (m, cols, entries, al)
            if m < 2:
                nc.scalar.copy(e_sb[m + 2][:, 512:1024], last[m + 2][:])
        finish(*waiting)
